import numpy as np
import ml_dtypes


def mxq(x, axis, fmt="e4m3"):
    dtype, down = {"e4m3": (ml_dtypes.float8_e4m3fn, 7), "e5m2": (ml_dtypes.float8_e5m2, 14)}[fmt]
    v = np.moveaxis(np.asarray(x, np.float32).astype(ml_dtypes.bfloat16).astype(np.float64), axis, -1)
    blocks = v.reshape(v.shape[:-1] + (-1, 32))
    amax = np.abs(blocks).max(-1, keepdims=True)
    byte = np.maximum(np.where(amax > 0, np.frexp(amax)[1] - 1 + 127, 0) - down, 1)
    scale = np.exp2(byte - 127.0)
    codes = (blocks / scale).astype(np.float32).astype(dtype).astype(np.float64)
    return np.moveaxis((codes * scale).reshape(v.shape), -1, axis)


WIDE = False


def mx_kscale(k):
    if not WIDE:
        return np.ones(k)
    levels = np.array([10, -10, 5, -5, 0])
    if k % 512:
        return np.exp2(np.random.permutation(np.resize(levels, k // 32))).repeat(32)
    a = np.empty((k // 512, 16))
    for p in range(k // 512):
        a[p, :8] = np.random.permutation(np.resize(levels, 8))
        for g in range(8):
            far = levels[np.abs(levels - a[p, g]) >= 10]
            a[p, g + 8] = far[np.random.randint(len(far))]
    return np.exp2(a.ravel()).repeat(32)


BF16 = ml_dtypes.bfloat16


def bf(x):
    return np.asarray(x, np.float32).astype(BF16)


def f64(x):
    return np.asarray(x).astype(np.float64)

def planes(Y):
    n, m = Y.shape
    b = f64(bf(Y)).reshape(n // 32, 32, m)
    amax = np.abs(b).max(1)
    byte = np.clip(np.where(amax > 0, np.frexp(amax)[1] - 1 + 127 - 7, 1), 1, 254)
    codes = (b * np.exp2(127.0 - byte)[:, None, :]).reshape(n, m).astype(np.float32).astype(ml_dtypes.float8_e4m3fn).view(np.uint8)
    words = codes.reshape(n // 512, 128, 4, m).transpose(0, 1, 3, 2)
    return np.ascontiguousarray(words), np.ascontiguousarray(byte.astype(np.uint8).reshape(n // 512, 16, m))


N, D, H = 1024, 1024, 1024

ALPHAS = (0.1127016653792583, 0.5, 0.8872983346207417)
OMEGAS = (5.0 / 18.0, 8.0 / 18.0, 5.0 / 18.0)


def tanh_at_node(u0, du, alpha, g, b):
    return np.tanh(g[None, :] * (u0 + alpha * du) + b[None, :])


def setup_inputs():
    s, t = mx_kscale(D), mx_kscale(H)
    return {
        "x": bf(np.random.standard_normal((N, D)) * s),
        "x0": bf(np.random.standard_normal((N, D)) * 0.5 * s),
        "w": bf(np.random.standard_normal((D, H)) / np.sqrt(D) / s[:, None] * t),
        "g": bf((1.0 + 0.1 * np.random.standard_normal(H)) / t),
        "b": bf(0.4 * np.random.standard_normal(H)),
        "v": bf(np.random.standard_normal(H)),
    }


def core(x, x0, w, g, b, v):
    x, x0, w, g, b, v = f64(x), f64(x0), f64(w), f64(g), f64(b), f64(v)

    wq = mxq(w, 0, "e4m3")
    u1 = mxq(x, 1, "e4m3") @ wq
    u0 = mxq(x0, 1, "e4m3") @ wq
    du = u1 - u0

    q_1 = tanh_at_node(u0, du, ALPHAS[0], g, b)
    q_2 = tanh_at_node(u0, du, ALPHAS[1], g, b)
    q_3 = tanh_at_node(u0, du, ALPHAS[2], g, b)

    m = OMEGAS[0] * (1.0 - q_1 * q_1) + OMEGAS[1] * (1.0 - q_2 * q_2) + OMEGAS[2] * (1.0 - q_3 * q_3)

    e = m * (v * g)[None, :]

    grad = mxq(e, 1, "e4m3") @ mxq(w, 1, "e4m3").T

    return (x - x0) * grad


def reference(x, x0, w, g, b, v):
    R_out = core(x, x0, w, g, b, v)
    words, scales = planes(R_out.T)
    return R_out, words, scales

from contextlib import ExitStack

import concourse.mybir as mybir
from concourse.masks import make_identity

N, D, H = 1024, 1024, 1024
FLOPS = 2 * 3 * N * D * H

F32 = mybir.dt.float32
BF16 = mybir.dt.bfloat16
U32 = mybir.dt.uint32
I32 = mybir.dt.int32
U8 = mybir.dt.uint8
FP8X4 = mybir.dt.float8_e4m3fn_x4
ALU = mybir.AluOpType
ACT = mybir.ActivationFunctionType

A1 = 0.1127016653792583
A3 = 0.8872983346207417
CHUNKS = (256, 512, 256)


def tile_gausslegendreintegratedgradientstanhnet_x1_kernel(tc, x, x0, w, g, b, v, out_0, out_1, out_2):
    nc = tc.nc
    with ExitStack() as ctx:
        keep = ctx.enter_context(tc.tile_pool(name="keep", bufs=1))
        work = ctx.enter_context(tc.tile_pool(name="work", bufs=2))
        psum = ctx.enter_context(tc.psum_pool(name="psum", bufs=1))
        ctx.enter_context(tc.manual_schedule())

        starts = [sum(CHUNKS[:i]) for i in range(len(CHUNKS))]
        iters = []
        first_iter = []
        for c, width in enumerate(CHUNKS):
            first_iter.append(len(iters))
            step = 512 // width
            for h in range(0, 8, step):
                iters.append((c, h, step))
        n_iter = len(iters)
        last_iter = first_iter[1:] + [n_iter]
        last_iter = [i - 1 for i in last_iter]

        def bank(tag, bufs):
            return psum.tile([128, 512], F32, name="ps_" + tag, tag=tag, bufs=bufs)

        ctile = keep.tile([128, 128], BF16, name="ctile")
        nc.vector.memset(ctile[:], 0.0)
        ident = keep.tile([128, 128], F32, name="ident")
        make_identity(nc, ident[:])

        xt = {}

        def load_rows(name, src, i):
            t = keep.tile([128, D], BF16, name="%s_rows%d" % (name, i), align_bytes=64)
            nc.sync.dma_start(out=t[:], in_=src[128 * i : 128 * i + 128, :])
            xt[name, i] = t

        wn = {}

        def load_w(gh, gd):
            t = keep.tile([128, 4, 512], BF16, name="w_rows%d%d" % (gd, gh), align_bytes=64)
            nc.sync.dma_start(
                out=t[:],
                in_=w[512 * gd : 512 * gd + 512, 512 * gh : 512 * gh + 512].rearrange("(p j) h -> p j h", j=4),
            )
            wn[gd, gh] = t

        for i in (0, 1):
            load_rows("x0", x0, i)
        for gd in (0, 1):
            load_w(0, gd)
        for i in (0, 1):
            load_rows("x", x, i)
        for r, vec in enumerate((g, b, v)):
            nc.sync.dma_start(out=ctile[8 * r : 8 * r + 8, :], in_=vec.rearrange("(c p) -> c p", p=128))
        for gd in (0, 1):
            load_w(1, gd)
        for i in range(2, 6):
            load_rows("x0", x0, i)
        for i in range(2, 6):
            load_rows("x", x, i)
        for i in (6, 7):
            load_rows("x0", x0, i)
        for i in (6, 7):
            load_rows("x", x, i)

        xg = {}
        xcode = {}
        xscale = {}

        def x_alloc(c, name):
            xg[c, name] = work.tile([128, 2, CHUNKS[c], 2], F32, name="xg", tag="grp", bufs=2, align_bytes=64)
            xcode[c, name] = keep.tile([128, 2, CHUNKS[c]], U32, name="%scode%d" % (name, c), align_bytes=64)
            xscale[c, name] = keep.tile([128, 2, CHUNKS[c]], U8, name="%sscale%d" % (name, c), align_bytes=64)

        def words_of(t):
            return t.bitcast(F32)

        def x_turn(c, name, i):
            m = bank("m", 4)
            wv = xt[name, starts[c] // 128 + i][:].bitcast(F32)
            for gd in (0, 1):
                for u in (0, 1):
                    j = 2 * gd + u
                    nc.tensor.transpose(
                        m[:, 128 * j : 128 * j + 128], wv[:, 256 * gd + u : 256 * gd + 256 : 2], ident[:]
                    )
            return m

        def x_copy(copy, c, name, i, m):
            copy(
                out=xg[c, name][:, :, 128 * i : 128 * i + 128, :],
                in_=m[:].rearrange("p (g u n) -> p g n u", g=2, u=2),
            )

        def x_quant(c, name, gd):
            nc.vector.quantize_mx(
                out=xcode[c, name][:, gd, :].bitcast(FP8X4),
                scales=xscale[c, name][:, gd, :],
                in_=xg[c, name][:, gd, :, :].rearrange("p n u -> p (n u)").bitcast(BF16),
            )

        wg = {}
        wcode = {}
        wscale = {}
        for gh in (0, 1):
            wcode[gh] = keep.tile([128, 2, 512], U32, name="wcode%d" % gh, align_bytes=64)
            wscale[gh] = keep.tile([128, 2, 512], U8, name="wscale%d" % gh, align_bytes=64)

        def w_group(gh, gd):
            t = work.tile([128, 512, 4], BF16, name="wg", tag="grp4", bufs=4, align_bytes=64)
            nc.vector.tensor_copy(
                out=t[:].rearrange("p (c i) j -> p c j i", i=4),
                in_=wn[gd, gh][:].rearrange("p j (c i) -> p c j i", i=4),
            )
            wg[gd, gh] = t

        def w_quant(gh, gd):
            nc.vector.quantize_mx(
                out=wcode[gh][:, gd, :].bitcast(FP8X4),
                scales=wscale[gh][:, gd, :],
                in_=wg[gd, gh][:].rearrange("p h j -> p (h j)"),
            )

        wtg = {}
        wtcode = {}
        wtscale = {}

        def wt_alloc(gh, gd):
            wtg[gh, gd] = work.tile([128, 512, 2], F32, name="wtg", tag="grp4", bufs=4, align_bytes=64)
            wtcode[gh, gd] = keep.tile([128, 512], U32, name="wtcode%d%d" % (gh, gd), align_bytes=64)
            wtscale[gh, gd] = keep.tile([128, 512], U8, name="wtscale%d%d" % (gh, gd), align_bytes=64)

        def wt_turn(gh, gd, jj):
            m = bank("m", 4)
            wv = wn[gd, gh][:].rearrange("p j h -> p (j h)").bitcast(F32)
            for j in (0, 1):
                for u in (0, 1):
                    k = 2 * j + u
                    at = 256 * (2 * jj + j)
                    nc.tensor.transpose(m[:, 128 * k : 128 * k + 128], wv[:, at + u : at + 256 : 2], ident[:])
            return m

        def wt_copy(copy, gh, gd, jj, m):
            copy(
                out=wtg[gh, gd][:, 256 * jj : 256 * jj + 256, :].rearrange("p (j q) u -> p j q u", j=2),
                in_=m[:].rearrange("p (j u q) -> p j q u", j=2, u=2),
            )

        def wt_quant(gh, gd):
            nc.vector.quantize_mx(
                out=wtcode[gh, gd][:].bitcast(FP8X4),
                scales=wtscale[gh, gd][:],
                in_=wtg[gh, gd][:].rearrange("p q u -> p (q u)").bitcast(BF16),
            )

        ubank = {}
        u0s = {}
        zt = {}
        qt = {}
        st = {}
        pb = {}

        def stage1(k, name):
            c, h0, step = iters[k]
            width = CHUNKS[c]
            m = bank(name, 2 if name == "u1" else 1)
            src = "x" if name == "u1" else "x0"
            for i in range(step):
                h = h0 + i
                gh, col = h // 4, 128 * (h % 4)
                for gd in (0, 1):
                    nc.tensor.matmul_mx(
                        out=m[:, width * i : width * i + width],
                        lhsT=wcode[gh][:, gd, col : col + 128].bitcast(FP8X4),
                        lhsT_scale=wscale[gh][:, gd, col : col + 128],
                        rhs=xcode[c, src][:, gd, :].bitcast(FP8X4),
                        rhs_scale=xscale[c, src][:, gd, :],
                        start=(gd == 0),
                        stop=(gd == 1),
                    )
            ubank[name, k] = m

        def u0_copy(k):
            t = work.tile([128, 512], F32, name="u0s", tag="u0s", bufs=2)
            nc.scalar.copy(out=t[:], in_=ubank["u0", k][:])
            u0s[k] = t
            zt[k] = work.tile([128, 3, 512], F32, name="zt", tag="zt", bufs=2)

        def z_make(k, node):
            u1b = ubank["u1", k]
            if node == 1:
                nc.vector.tensor_tensor(out=zt[k][:, 1, :], in0=u1b[:], in1=u0s[k][:], op=ALU.add)
            else:
                r = A3 / A1 if node == 0 else A1 / A3
                nc.vector.scalar_tensor_tensor(
                    out=zt[k][:, node, :], in0=u0s[k][:], scalar=r, in1=u1b[:], op0=ALU.mult, op1=ALU.add
                )

        def tanh(k, node):
            c, h0, step = iters[k]
            width = CHUNKS[c]
            if node == 0:
                qt[k] = work.tile([128, 3, 512], F32, name="qt", tag="qt", bufs=2)
                st[k] = work.tile([128, 3, 512], F32, name="st", tag="st", bufs=2)
            for i in range(step):
                h = h0 + i
                nc.scalar.activation(
                    out=qt[k][:, node, width * i : width * i + width],
                    in_=zt[k][:, node, width * i : width * i + width],
                    func=ACT.Tanh,
                    scale=gsc[:, node, h : h + 1],
                    bias=cols[:, 8 + h : 9 + h],
                )

        def square_mid(k):
            nc.scalar.activation(out=st[k][:, 1, :], in_=qt[k][:, 1, :], func=ACT.Square, scale=1.6**0.5)

        def square_end(k, node):
            nc.gpsimd.tensor_tensor(out=st[k][:, node, :], in0=qt[k][:, node, :], in1=qt[k][:, node, :], op=ALU.mult)

        def p_sum(k):
            c, h0, step = iters[k]
            width = CHUNKS[c]
            m = bank("p", 1)
            for nt in range(width // 128):
                for i in range(step):
                    o = 128 * (nt * step + i)
                    for node in (1, 0, 2):
                        nc.tensor.matmul(
                            out=m[:, o : o + 128],
                            lhsT=st[k][:, node, width * i + 128 * nt : width * i + 128 * nt + 128],
                            rhs=ident[:],
                            start=(node == 1),
                            stop=(node == 2),
                            is_transpose=True,
                        )
            pb[k] = m

        enat = {}

        def e_make(k):
            c, h0, step = iters[k]
            nts = CHUNKS[c] // 128
            if h0 == 0:
                enat[c] = work.tile([128, nts, H], BF16, name="enat", tag="enat", bufs=2, align_bytes=64)
            cols_h = slice(128 * h0, 128 * (h0 + step))
            nc.vector.scalar_tensor_tensor(
                out=enat[c][:, :, cols_h],
                in0=pb[k][:].rearrange("p (n h) -> p n h", n=nts),
                scalar=3.6,
                in1=nvg[:, cols_h].unsqueeze(1).to_broadcast([128, nts, 128 * step]),
                op0=ALU.subtract,
                op1=ALU.mult,
            )

        eg = {}
        ecode = {}
        escale = {}

        def e_turn(c, gh, pair):
            m = bank("m", 4)
            for n in (0, 1):
                wv = enat[c][:, 2 * pair + n, :].bitcast(F32)
                for u in (0, 1):
                    k = 2 * n + u
                    nc.tensor.transpose(
                        m[:, 128 * k : 128 * k + 128], wv[:, 256 * gh + u : 256 * gh + 256 : 2], ident[:]
                    )
            return m

        def e_alloc(c, gh):
            eg[c, gh] = work.tile([128, CHUNKS[c], 2], F32, name="eg", tag="grp4", bufs=4, align_bytes=64)
            ecode[c, gh] = work.tile([128, CHUNKS[c]], U32, name="ecode", tag="ecode", bufs=4, align_bytes=64)
            escale[c, gh] = work.tile([128, CHUNKS[c]], U8, name="escale", tag="escale", bufs=4, align_bytes=64)

        def e_copy(copy, c, gh, pair, m):
            copy(
                out=eg[c, gh][:, 256 * pair : 256 * pair + 256, :].rearrange("p (n q) u -> p n q u", n=2),
                in_=m[:].rearrange("p (n u q) -> p n q u", n=2, u=2),
            )

        def e_quant(c, gh):
            nc.vector.quantize_mx(
                out=ecode[c, gh][:].bitcast(FP8X4),
                scales=escale[c, gh][:],
                in_=eg[c, gh][:].rearrange("p q u -> p (q u)").bitcast(BF16),
            )

        xd = {}
        rt = {}
        rb = {}
        rg = {}
        gbank = {}

        def diff(i, half):
            if half == 0:
                xd[i] = work.tile([128, D], F32, name="xd", tag="xd", bufs=5)
            cs = slice(512 * half, 512 * half + 512)
            nc.gpsimd.tensor_tensor(out=xd[i][:, cs], in0=xt["x", i][:, cs], in1=xt["x0", i][:, cs], op=ALU.subtract)

        def grad(c, nt, gd):
            m = bank("m", 4)
            for gh in (0, 1):
                nc.tensor.matmul_mx(
                    out=m[:],
                    lhsT=ecode[c, gh][:, 128 * nt : 128 * nt + 128].bitcast(FP8X4),
                    lhsT_scale=escale[c, gh][:, 128 * nt : 128 * nt + 128],
                    rhs=wtcode[gh, gd][:].bitcast(FP8X4),
                    rhs_scale=wtscale[gh, gd][:],
                    start=(gh == 0),
                    stop=(gh == 1),
                )
            gbank[c, nt, gd] = m

        def r_make(c, nt, gd):
            i = starts[c] // 128 + nt
            if gd == 0:
                rt[i] = work.tile([128, D], F32, name="rt", tag="rt", bufs=2, align_bytes=64)
            cs = slice(512 * gd, 512 * gd + 512)
            nc.vector.tensor_tensor(
                out=rt[i][:, cs].rearrange("p (q j) -> p q j", j=4),
                in0=gbank[c, nt, gd][:].rearrange("p (j q) -> p q j", j=4),
                in1=xd[i][:, cs].rearrange("p (q j) -> p q j", j=4),
                op=ALU.mult,
            )

        def r_store(i):
            nc.sync.dma_start(out=out_0[128 * i : 128 * i + 128, :], in_=rt[i][:])

        def r_round(i):
            rb[i] = work.tile([128, D], BF16, name="rb", tag="rb", bufs=3, align_bytes=64)
            nc.vector.tensor_copy(out=rb[i][:], in_=rt[i][:])

        def r_turn(i):
            m = bank("m", 4)
            wv = rb[i][:].bitcast(F32)
            for gd in (0, 1):
                for u in (0, 1):
                    k = 2 * gd + u
                    nc.tensor.transpose(
                        m[:, 128 * k : 128 * k + 128], wv[:, 256 * gd + u : 256 * gd + 256 : 2], ident[:]
                    )
            return m

        def r_copy(copy, i, m):
            pair = i // 2
            if i % 2 == 0:
                rg[pair] = work.tile([128, 2, 256, 2], F32, name="rg", tag="grp4", bufs=4, align_bytes=64)
            o = 128 * (i % 2)
            copy(out=rg[pair][:, :, o : o + 128, :], in_=m[:].rearrange("p (g u n) -> p g n u", g=2, u=2))

        def r_quant(pair):
            code = work.tile([128, 2, 256], U32, name="rcode", tag="rcode", bufs=2, align_bytes=64)
            scale = work.tile([128, 2, 256], U8, name="rscale", tag="rscale", bufs=2, align_bytes=64)
            for gd in (0, 1):
                nc.vector.quantize_mx(
                    out=code[:, gd, :].bitcast(FP8X4),
                    scales=scale[:, gd, :],
                    in_=rg[pair][:, gd, :, :].rearrange("p n u -> p (n u)").bitcast(BF16),
                )
            ns = slice(256 * pair, 256 * pair + 256)
            nc.sync.dma_start(
                out=out_1[:, :, ns, :].rearrange("g p m t -> p g (m t)").bitcast(I32), in_=code[:].bitcast(I32)
            )
            for quad in range(4):
                nc.sync.dma_start(
                    out=out_2[:, 4 * quad : 4 * quad + 4, ns].rearrange("g r n -> r g n").bitcast(I32),
                    in_=scale[32 * quad : 32 * quad + 4, :, :].bitcast(I32),
                )

        slots = n_iter + 16
        todo = {}
        for name in ("mx", "turn", "s", "v", "v2", "g"):
            todo[name] = [[] for s in range(slots)]

        def put(queue, slot, fn, *args):
            todo[queue][slot].append((fn, args))

        def run(queue, slot):
            for fn, args in todo[queue][slot]:
                fn(*args)

        held = {}

        def turn_and_copy(slot, turn, copy, args, engine="s"):
            def do_turn():
                held[turn, args] = turn(*args)

            def do_copy():
                eng = nc.scalar.copy if engine == "s" else nc.vector.tensor_copy
                copy(eng, *args, held[turn, args])

            put("turn", slot, do_turn)
            put("s" if engine == "s" else "v2", slot, do_copy)

        for gd in (0, 1):
            put("v", 0, w_group, 1, gd)
        for gd in (0, 1):
            put("v", 0, w_quant, 1, gd)
        put("s", 0, x_alloc, 1, "x0")
        put("s", 0, x_alloc, 1, "x")
        for j, (name, i) in enumerate([(nm, i) for nm in ("x0", "x") for i in range(4)]):
            turn_and_copy(min(2, j // 3), x_turn, x_copy, (1, name, i))
        for gd in (0, 1):
            put("v", 2, x_quant, 1, "x0", gd)
        for gd in (0, 1):
            put("v", 3, x_quant, 1, "x", gd)
        wt_units = [(gh, gd, jj) for gd in (0, 1) for gh in (0, 1) for jj in (0, 1)]
        for j, unit in enumerate(wt_units):
            slot = 3 + j // 2
            if unit[2] == 0:
                put("s", slot, wt_alloc, unit[0], unit[1])
            turn_and_copy(slot, wt_turn, wt_copy, unit)
            if unit[2] == 1:
                put("v", slot + 1, wt_quant, unit[0], unit[1])
        put("s", 7, x_alloc, 2, "x0")
        put("s", 7, x_alloc, 2, "x")
        for j, (name, i) in enumerate([(nm, i) for nm in ("x0", "x") for i in range(2)]):
            turn_and_copy(7 + j, x_turn, x_copy, (2, name, i))
        for gd in (0, 1):
            put("v", 9, x_quant, 2, "x0", gd)
        for gd in (0, 1):
            put("v", 11, x_quant, 2, "x", gd)
        for j in range(16):
            put("g", 3 + j, diff, j // 2, j % 2)
        begin = {0: 8, 1: last_iter[1] + 3, 2: last_iter[2] + 3}
        for c, width in enumerate(CHUNKS):
            pairs = width // 256
            for gh in (0, 1):
                if gh == 0:
                    slot = first_iter[c] + (last_iter[c] + 1 - first_iter[c]) // 2 - 1 + 3
                else:
                    slot = last_iter[c] + 3
                put("s", slot, e_alloc, c, gh)
                for pair in range(pairs):
                    turn_and_copy(slot, e_turn, e_copy, (c, gh, pair))
                put("v", slot + 1, e_quant, c, gh)
            s0 = begin[c] + 1
            for nt in range(width // 128):
                i = starts[c] // 128 + nt
                for gd in (0, 1):
                    put("mx", s0 + nt, grad, c, nt, gd)
                    put("v2", s0 + nt, r_make, c, nt, gd)
                put("v2", s0 + nt, r_store, i)
                put("v", s0 + nt + 1, r_round, i)
                turn_and_copy(s0 + nt + 1, r_turn, r_copy, (i,))
                if i % 2 == 1:
                    put("v", s0 + nt + 2, r_quant, i // 2)

        cf = keep.tile([128, 128], F32, name="cf")
        cols = keep.tile([128, 24], F32, name="cols")
        gsc = keep.tile([128, 3, 8], F32, name="gsc")
        nvgc = keep.tile([128, 8], F32, name="nvgc")
        nvg = keep.tile([128, H], F32, name="nvg")

        x_alloc(0, "x0")
        x_alloc(0, "x")
        for i in (0, 1):
            m = x_turn(0, "x0", i)
            x_copy(nc.scalar.copy, 0, "x0", i, m)
        for gd in (0, 1):
            w_group(0, gd)
        for gd in (0, 1):
            w_quant(0, gd)
        for gd in (0, 1):
            x_quant(0, "x0", gd)
        for i in (0, 1):
            m = x_turn(0, "x", i)
            x_copy(nc.scalar.copy, 0, "x", i, m)
        for gd in (0, 1):
            x_quant(0, "x", gd)
        nc.vector.tensor_copy(out=cf[:], in_=ctile[:])
        cps = bank("m", 4)
        nc.tensor.transpose(cps[:, 0:128], cf[:], ident[:])
        nc.scalar.copy(out=cols[:], in_=cps[:, 0:24])
        stage1(0, "u1")
        stage1(0, "u0")
        for node, alpha in enumerate((A1, 0.5, A3)):
            nc.vector.tensor_scalar(out=gsc[:, node, :], in0=cols[:, 0:8], scalar1=alpha, scalar2=None, op0=ALU.mult)
        nc.vector.scalar_tensor_tensor(
            out=nvgc[:], in0=cols[:, 0:8], scalar=-5.0 / 18.0, in1=cols[:, 16:24], op0=ALU.mult, op1=ALU.mult
        )
        nvg_banks = []
        for half in (0, 1):
            m = bank("m", 4)
            for i in range(4):
                h = 4 * half + i
                nc.tensor.transpose(
                    m[:, 128 * i : 128 * i + 128], nvgc[:, h : h + 1].to_broadcast([128, 128]), ident[:]
                )
            nvg_banks.append(m)
        for half in (0, 1):
            put("s", 0, nc.scalar.copy, nvg[:, 512 * half : 512 * half + 512], nvg_banks[half][:])

        for s in range(slots):
            if s < n_iter:
                u0_copy(s)
            if 3 <= s < n_iter + 3:
                e_make(s - 3)
            run("v", s)
            if s + 1 < n_iter:
                stage1(s + 1, "u1")
            run("mx", s)
            if s + 1 < n_iter:
                stage1(s + 1, "u0")
            if s < n_iter:
                for node in (0, 2, 1):
                    z_make(s, node)
            run("g", s)
            if 1 <= s < n_iter + 1:
                tanh(s - 1, 0)
                square_end(s - 1, 0)
                tanh(s - 1, 2)
                square_end(s - 1, 2)
                tanh(s - 1, 1)
                square_mid(s - 1)
            if 2 <= s < n_iter + 2:
                p_sum(s - 2)
            run("turn", s)
            run("s", s)
            run("v2", s)
